import numpy as np, ml_dtypes
CORES = [25,29,65,69,153,157,193,197]
N = 8
import mx_ref
NC, KT, ROOT = 128, 4, 3
BF = ml_dtypes.bfloat16
def setup_inputs(rng):
    def f(*shape):
        return mx_ref.flush((rng.standard_normal(shape, dtype=np.float32) * np.exp2(rng.integers(-2, 3, shape[:-1] + (1,)))).astype(BF))
    return {"w": f(N, 128, KT * 512), "x": f(N, 128, KT * 4 * NC)}
def setup_inputs_blocks(rng):
    d = setup_inputs(rng)
    for k in ("w", "x"): d[k] = mx_ref.spread(d[k], rng, 1)
    return d
def setup_inputs_wide(rng):
    d = setup_inputs(rng)
    for k in ("w", "x"): d[k] = mx_ref.flush((d[k].astype(np.float32) * np.exp2(rng.integers(-8, 9, (N, 1, 1))).astype(np.float32)).astype(BF))
    return d
def setup_inputs_zeros(rng):
    d = setup_inputs(rng); v = d["x"].reshape(N, 128, -1, 4).copy()
    v[np.broadcast_to((rng.random((N, 1, v.shape[2], 1)) < 0.33), v.shape)] = 0
    d["x"] = v.reshape(d["x"].shape)
    return d
def reference(w, x):
    QW = [mx_ref.quantize(w[ROOT][:, 512 * t:512 * t + 512]) for t in range(KT)]
    y = np.zeros((N, 128, NC), np.float32)
    for r in range(N):
        for t in range(KT):
            p = mx_ref.matmul(QW[t], mx_ref.quantize(x[r][:, 4 * NC * t:4 * NC * t + 4 * NC]))
            y[r] = p if t == 0 else y[r] + p
    return {"y": y}

@@ -1,0 +1,139 @@
+from concourse.bass import DstId, RemoteDMATransfer
+from concourse.mybir import dt
+
+KT, TW = 4, 128
+NW = KT * TW
+H = NW // 2
+
+SCRATCH = {
+    "wb": ("sbuf", [128, 4 * NW], "bfloat16"),
+    "xb": ("sbuf", [128, 4 * NW], "bfloat16"),
+    "wq": ("sbuf", [128, NW], "float8_e4m3fn_x4"),
+    "ws": ("sbuf", [128, NW], "uint8"),
+    "xq": ("sbuf", [128, NW], "float8_e4m3fn_x4"),
+    "xs": ("sbuf", [128, NW], "uint8"),
+    "acc": ("psum", [128, 512], "float32"),
+    "yo": ("sbuf", [128, TW], "float32"),
+}
+SEMAPHORES = ["c0", "c1", "s0", "s1", "cf", "sf", "wl0", "wl1", "q0", "q1", "xl", "xqd", "mm", "cp", "st", "sent"]
+
+
+def build_plan(T, topo):
+    root = T.cores[T.root]
+    world = range((1 + max(topo.host(c) for c in T.cores)) * topo.CORES_PER_HOST)
+    home = [c for c in world if c != root and topo.host(c) == topo.host(root) and topo.chip(c) == topo.chip(root)]
+    beside = [c for c in T.cores if c in home][0]
+    plane = [c for c in T.cores if topo.same_plane(root, c)]
+    far = [c for c in T.cores if c != root and not topo.may_write(root, c)]
+    relays = [c for c in home if c not in T.cores and all(topo.may_write(c, d) for d in far)]
+    dies = sorted(set(topo.die(c) for c in far), key=lambda d: d != topo.die(root))
+    rel = {d: [c for c in relays if topo.die(c) == d] for d in dies}
+    fard = {d: [c for c in far if topo.die(c) == d] for d in dies}
+    direct = [c for c in plane if topo.die(c) == topo.die(root)]
+    passed = [c for c in plane if topo.die(c) == topo.die(beside)]
+    r0, r1 = [rel[d][0] for d in dies], [rel[d][1] for d in dies]
+    stages = [(0, H), (H, NW)]
+    calls = [
+        (root, ["q0"], [("c", 0, H, r0, "c0")]),
+        (root, [], [("s", 0, H, r1 + [beside], "s0")]),
+        (root, ["q1"], [("c", H, NW, r1, "c1")]),
+        (root, [], [("s", H, NW, r0 + [beside], "s1")]),
+        (root, [], [("c", 0, NW, [beside], "cf")]),
+        (root, [], [("c", 0, NW, direct, "cf")]),
+        (root, [], [("s", 0, NW, direct, "sf")]),
+        (beside, ["s0"], [("s", 0, H, passed, "s0")]),
+        (beside, ["s1"], [("s", H, NW, passed, "s1")]),
+        (beside, ["cf"], [("c", 0, NW, passed, "cf")]),
+    ]
+    for d in dies:
+        calls += [
+            (rel[d][0], ["c0"], [("c", 0, H, fard[d], "c0")]),
+            (rel[d][0], ["s1"], [("s", H, NW, fard[d], "s1")]),
+            (rel[d][1], ["s0"], [("s", 0, H, fard[d], "s0")]),
+            (rel[d][1], ["c1"], [("c", H, NW, fard[d], "c1")]),
+        ]
+    return root, stages, calls
+
+
+def engines(topo, src, dsts):
+    m = topo.mask(src, dsts[0])
+    for d in dsts:
+        m &= topo.mask(src, d)
+    return m, sum(m >> e & 1 for e in range(m.bit_length()))
+
+
+def rank_program(g, core, T, topo):
+    root, stages, calls = build_plan(T, topo)
+    rank = T.rank_of(core)
+
+    def view(kind, a, b):
+        return T.wq[:, a:b].bitcast(dt.uint8) if kind == "c" else T.ws[:, a:b]
+
+    expect, cover = {}, []
+    for src, need, xf in calls:
+        for kind, a, b, dsts, grp in xf:
+            if core in dsts:
+                expect[grp] = expect.get(grp, 0) + engines(topo, src, dsts)[1]
+                cover.append((a, b, grp))
+    mine = [c for c in calls if c[0] == core]
+    if rank is None and not mine:
+        return
+
+    if core == root:
+        for k, (a, b) in enumerate(stages):
+            q = g.sync if k % 2 == 0 else g.scalar
+            q.dma_start(T.wb[:, 4 * a:4 * b], T.w[:, 4 * a:4 * b]).then_inc(T.sem["wl%d" % k], 16)
+        for k, (a, b) in enumerate(stages):
+            g.vector.wait_ge(T.sem["wl%d" % k], 16)
+            g.vector.quantize_mx(T.wq[:, a:b], T.ws[:, a:b], T.wb[:, 4 * a:4 * b]).then_inc(T.sem["q%d" % k], 1)
+    if rank is not None:
+        g.sync.dma_start(T.xb[:], T.x[:]).then_inc(T.sem.xl, 16)
+        g.vector.wait_ge(T.sem.xl, 16)
+        g.vector.quantize_mx(T.xq[:], T.xs[:], T.xb[:]).then_inc(T.sem.xqd, 1)
+
+    left = 0
+    for src, need, xf in mine:
+        for s in need:
+            g.wait_ge(T.sem[s], 1 if core == root else expect[s])
+        trs = []
+        for kind, a, b, dsts, grp in xf:
+            m, n = engines(topo, core, dsts)
+            ids = []
+            for d in dsts:
+                rid, pid = topo.addr(d, core)
+                ids.append(DstId(rid=rid, pnc=pid))
+            trs.append(RemoteDMATransfer(dst_ids=ids, dma_engine_mask=m, remote_sem=T.sem[grp],
+                                         srcs=[view(kind, a, b)], dsts=[view(kind, a, b) for d in dsts]))
+            left += n
+        g.remote_dma_fused(trs, local_sem=T.sem.sent)
+    if left:
+        g.wait_ge(T.sem.sent, left)
+    if rank is None:
+        return
+
+    te = g.tensor
+    te.wait_ge(T.sem.xqd, 1)
+    order = []
+    for t in range(KT):
+        a, b = t * TW, (t + 1) * TW
+        if core == root:
+            needs = [(k, "q%d" % k, 1) for k, (sa, sb) in enumerate(stages) if sa < b and a < sb]
+        else:
+            needs = [(i, grp, expect[grp]) for i, (ca, cb, grp) in enumerate(cover) if ca < b and a < cb]
+        order.append((max(needs)[0], t, needs))
+    order.sort()
+    seen = set()
+    last = None
+    for j, (_, t, needs) in enumerate(order):
+        for _i, s, v in needs:
+            if s not in seen:
+                seen.add(s)
+                te.wait_ge(T.sem[s], v)
+        a, b = t * TW, (t + 1) * TW
+        last = te.matmul_mx(T.acc[:, 0:TW], T.wq[:, a:b], T.ws[:, a:b], T.xq[:, a:b], T.xs[:, a:b], j == 0, j == KT - 1)
+    last.then_inc(T.sem.mm, 1)
+    g.vector.wait_ge(T.sem.mm, 1)
+    g.vector.tensor_copy(T.yo[:], T.acc[:, 0:TW]).then_inc(T.sem.cp, 1)
+    g.sync.wait_ge(T.sem.cp, 1)
+    g.sync.dma_start(T.y[:], T.yo[:]).then_inc(T.sem.st, 16)
+    g.sync.wait_ge(T.sem.st, 16)

@@ -4,6 +4,7 @@ from concourse.mybir import dt
 KT, TW = 4, 128
 NW = KT * TW
 H = NW // 2
+HALVES = [(0, H), (H, NW)]
 
 SCRATCH = {
     "wb": ("sbuf", [128, 4 * NW], "bfloat16"),
@@ -15,55 +16,73 @@ SCRATCH = {
     "acc": ("psum", [128, 512], "float32"),
     "yo": ("sbuf", [128, TW], "float32"),
 }
-SEMAPHORES = ["c0", "c1", "s0", "s1", "cf", "sf", "wl0", "wl1", "q0", "q1", "xl", "xqd", "mm", "cp", "st", "sent"]
+SEMAPHORES = ["c0", "c1", "s0", "s1", "wl0", "wl1", "q0", "q1", "xl0", "xl1", "xq0", "xq1", "go", "mm", "cp", "st", "sent"]
+
+
+def piece(kind, h, dsts):
+    a, b = HALVES[h]
+    return (kind, a, b, dsts, "%s%d" % (kind, h))
 
 
 def build_plan(T, topo):
     root = T.cores[T.root]
+
+    def place(c):
+        return (topo.host(c), topo.chip(c))
+
     world = range((1 + max(topo.host(c) for c in T.cores)) * topo.CORES_PER_HOST)
-    home = [c for c in world if c != root and topo.host(c) == topo.host(root) and topo.chip(c) == topo.chip(root)]
+    home = [c for c in world if c != root and place(c) == place(root)]
     beside = [c for c in T.cores if c in home][0]
-    plane = [c for c in T.cores if topo.same_plane(root, c)]
     far = [c for c in T.cores if c != root and not topo.may_write(root, c)]
     relays = [c for c in home if c not in T.cores and all(topo.may_write(c, d) for d in far)]
-    dies = sorted(set(topo.die(c) for c in far), key=lambda d: d != topo.die(root))
-    rel = {d: [c for c in relays if topo.die(c) == d] for d in dies}
-    fard = {d: [c for c in far if topo.die(c) == d] for d in dies}
-    direct = [c for c in plane if topo.die(c) == topo.die(root)]
-    passed = [c for c in plane if topo.die(c) == topo.die(beside)]
-    r0, r1 = [rel[d][0] for d in dies], [rel[d][1] for d in dies]
-    stages = [(0, H), (H, NW)]
+    dr, db = topo.die(root), topo.die(beside)
+    half = {db: 0, dr: 1}
+    rel = {d: [c for c in relays if topo.die(c) == d] for d in half}
+    chips = sorted(set(place(c) for c in T.cores if place(c) != place(root)))
+    on = {k: {topo.die(c): c for c in T.cores if place(c) == k} for k in chips}
+    farchips = [k for k in chips if on[k][dr] in far]
+    near = [k for k in chips if k not in farchips]
+    carrier = {}
+    for i, k in enumerate(farchips):
+        for d in half:
+            carrier[k, d] = rel[d][i]
+    for k in near:
+        carrier[k, dr], carrier[k, db] = root, beside
+    fed = {d: [carrier[k, d] for k in farchips] for d in half}
+    direct = [on[k][dr] for k in near]
     calls = [
-        (root, ["q0"], [("c", 0, H, r0, "c0")]),
-        (root, [], [("s", 0, H, r1 + [beside], "s0")]),
-        (root, ["q1"], [("c", H, NW, r1, "c1")]),
-        (root, [], [("s", H, NW, r0 + [beside], "s1")]),
-        (root, [], [("c", 0, NW, [beside], "cf")]),
-        (root, [], [("c", 0, NW, direct, "cf")]),
-        (root, [], [("s", 0, NW, direct, "sf")]),
-        (beside, ["s0"], [("s", 0, H, passed, "s0")]),
-        (beside, ["s1"], [("s", H, NW, passed, "s1")]),
-        (beside, ["cf"], [("c", 0, NW, passed, "cf")]),
+        (root, ["q0"], [piece("s", 0, fed[db] + [beside])]),
+        (root, ["q1"], [piece("s", 1, fed[dr])]),
+        (root, [], [piece("c", 0, fed[db] + [beside])]),
+        (root, [], [piece("c", 1, fed[dr])]),
+        (root, [], [piece("s", 1, direct), piece("s", 1, [beside])]),
+        (root, [], [piece("c", 1, direct), piece("c", 1, [beside])]),
     ]
-    for d in dies:
-        calls += [
-            (rel[d][0], ["c0"], [("c", 0, H, fard[d], "c0")]),
-            (rel[d][0], ["s1"], [("s", H, NW, fard[d], "s1")]),
-            (rel[d][1], ["s0"], [("s", 0, H, fard[d], "s0")]),
-            (rel[d][1], ["c1"], [("c", H, NW, fard[d], "c1")]),
-        ]
-    return root, stages, calls
+    for kind in "sc":
+        for (k, d), c in sorted(carrier.items()):
+            if c != root:
+                calls.append((c, ["%s%d" % (kind, half[d])], [piece(kind, half[d], [on[k][d]])]))
+    for kind in "sc":
+        for k in chips:
+            for d, o in ((db, dr), (dr, db)):
+                calls.append((on[k][d], ["%s%d" % (kind, half[d])], [piece(kind, half[d], [on[k][o]])]))
+    return root, calls
 
 
-def engines(topo, src, dsts):
-    m = topo.mask(src, dsts[0])
-    for d in dsts:
-        m &= topo.mask(src, d)
-    return m, sum(m >> e & 1 for e in range(m.bit_length()))
+def masks(topo, src, xf):
+    used, out = 0, []
+    for kind, a, b, dsts, grp in xf:
+        m = topo.mask(src, dsts[0])
+        for d in dsts:
+            m &= topo.mask(src, d)
+        m &= ~used
+        used |= m
+        out.append((m, sum(m >> e & 1 for e in range(m.bit_length()))))
+    return out
 
 
 def rank_program(g, core, T, topo):
-    root, stages, calls = build_plan(T, topo)
+    root, calls = build_plan(T, topo)
     rank = T.rank_of(core)
 
     def view(kind, a, b):
@@ -71,33 +90,37 @@ def rank_program(g, core, T, topo):
 
     expect, cover = {}, []
     for src, need, xf in calls:
-        for kind, a, b, dsts, grp in xf:
+        for (kind, a, b, dsts, grp), (m, n) in zip(xf, masks(topo, src, xf)):
             if core in dsts:
-                expect[grp] = expect.get(grp, 0) + engines(topo, src, dsts)[1]
+                expect[grp] = expect.get(grp, 0) + n
                 cover.append((a, b, grp))
     mine = [c for c in calls if c[0] == core]
     if rank is None and not mine:
         return
 
+    xst = HALVES if core == root else [(0, NW)]
     if core == root:
-        for k, (a, b) in enumerate(stages):
+        for k, (a, b) in enumerate(HALVES):
             q = g.sync if k % 2 == 0 else g.scalar
             q.dma_start(T.wb[:, 4 * a:4 * b], T.w[:, 4 * a:4 * b]).then_inc(T.sem["wl%d" % k], 16)
-        for k, (a, b) in enumerate(stages):
+        for k, (a, b) in enumerate(HALVES):
             g.vector.wait_ge(T.sem["wl%d" % k], 16)
             g.vector.quantize_mx(T.wq[:, a:b], T.ws[:, a:b], T.wb[:, 4 * a:4 * b]).then_inc(T.sem["q%d" % k], 1)
     if rank is not None:
-        g.sync.dma_start(T.xb[:], T.x[:]).then_inc(T.sem.xl, 16)
-        g.vector.wait_ge(T.sem.xl, 16)
-        g.vector.quantize_mx(T.xq[:], T.xs[:], T.xb[:]).then_inc(T.sem.xqd, 1)
+        for k, (a, b) in enumerate(xst):
+            if core == root and k == len(xst) - 1:
+                g.sync.wait_ge(T.sem.go, 1)
+            g.sync.dma_start(T.xb[:, 4 * a:4 * b], T.x[:, 4 * a:4 * b]).then_inc(T.sem["xl%d" % k], 16)
+        for k, (a, b) in enumerate(xst):
+            g.vector.wait_ge(T.sem["xl%d" % k], 16)
+            g.vector.quantize_mx(T.xq[:, a:b], T.xs[:, a:b], T.xb[:, 4 * a:4 * b]).then_inc(T.sem["xq%d" % k], 1)
 
     left = 0
     for src, need, xf in mine:
         for s in need:
             g.wait_ge(T.sem[s], 1 if core == root else expect[s])
         trs = []
-        for kind, a, b, dsts, grp in xf:
-            m, n = engines(topo, core, dsts)
+        for (kind, a, b, dsts, grp), (m, n) in zip(xf, masks(topo, core, xf)):
             ids = []
             for d in dsts:
                 rid, pid = topo.addr(d, core)
@@ -106,21 +129,24 @@ def rank_program(g, core, T, topo):
                                          srcs=[view(kind, a, b)], dsts=[view(kind, a, b) for d in dsts]))
             left += n
         g.remote_dma_fused(trs, local_sem=T.sem.sent)
+    if core == root:
+        g.sem_inc(T.sem.go, 1)
     if left:
         g.wait_ge(T.sem.sent, left)
     if rank is None:
         return
 
     te = g.tensor
-    te.wait_ge(T.sem.xqd, 1)
     order = []
     for t in range(KT):
         a, b = t * TW, (t + 1) * TW
         if core == root:
-            needs = [(k, "q%d" % k, 1) for k, (sa, sb) in enumerate(stages) if sa < b and a < sb]
+            needs = [(k, "q%d" % k, 1) for k, (sa, sb) in enumerate(HALVES) if sa < b and a < sb]
         else:
             needs = [(i, grp, expect[grp]) for i, (ca, cb, grp) in enumerate(cover) if ca < b and a < cb]
-        order.append((max(needs)[0], t, needs))
+        first = max(needs)[0]
+        needs = needs + [(k, "xq%d" % k, 1) for k, (sa, sb) in enumerate(xst) if sa < b and a < sb]
+        order.append((first, t, needs))
     order.sort()
     seen = set()
     last = None

from concourse.bass import DstId, RemoteDMATransfer
from concourse.mybir import dt

KT, TW = 4, 128
NW = KT * TW
H = NW // 2
HALVES = [(0, H), (H, NW)]

SCRATCH = {
    "wb": ("sbuf", [128, 4 * NW], "bfloat16"),
    "xb": ("sbuf", [128, 4 * NW], "bfloat16"),
    "wq": ("sbuf", [128, NW], "float8_e4m3fn_x4"),
    "ws": ("sbuf", [128, NW], "uint8"),
    "xq": ("sbuf", [128, NW], "float8_e4m3fn_x4"),
    "xs": ("sbuf", [128, NW], "uint8"),
    "acc": ("psum", [128, 512], "float32"),
    "yo": ("sbuf", [128, TW], "float32"),
}
SEMAPHORES = ["c0", "c1", "s0", "s1", "wl0", "wl1", "q0", "q1", "xl0", "xl1", "xq0", "xq1", "go", "mm", "cp", "st", "sent"]


def piece(kind, h, dsts):
    a, b = HALVES[h]
    return (kind, a, b, dsts, "%s%d" % (kind, h))


def build_plan(T, topo):
    root = T.cores[T.root]

    def place(c):
        return (topo.host(c), topo.chip(c))

    world = range((1 + max(topo.host(c) for c in T.cores)) * topo.CORES_PER_HOST)
    home = [c for c in world if c != root and place(c) == place(root)]
    beside = [c for c in T.cores if c in home][0]
    far = [c for c in T.cores if c != root and not topo.may_write(root, c)]
    relays = [c for c in home if c not in T.cores and all(topo.may_write(c, d) for d in far)]
    dr, db = topo.die(root), topo.die(beside)
    half = {db: 0, dr: 1}
    rel = {d: [c for c in relays if topo.die(c) == d] for d in half}
    chips = sorted(set(place(c) for c in T.cores if place(c) != place(root)))
    on = {k: {topo.die(c): c for c in T.cores if place(c) == k} for k in chips}
    farchips = [k for k in chips if on[k][dr] in far]
    near = [k for k in chips if k not in farchips]
    carrier = {}
    for i, k in enumerate(farchips):
        for d in half:
            carrier[k, d] = rel[d][i]
    for k in near:
        carrier[k, dr], carrier[k, db] = root, beside
    fed = {d: [carrier[k, d] for k in farchips] for d in half}
    direct = [on[k][dr] for k in near]
    calls = [
        (root, ["q0"], [piece("s", 0, fed[db] + [beside])]),
        (root, ["q1"], [piece("s", 1, fed[dr])]),
        (root, [], [piece("c", 0, fed[db] + [beside])]),
        (root, [], [piece("c", 1, fed[dr])]),
        (root, [], [piece("s", 1, direct), piece("s", 1, [beside])]),
        (root, [], [piece("c", 1, direct), piece("c", 1, [beside])]),
    ]
    for kind in "sc":
        for (k, d), c in sorted(carrier.items()):
            if c != root:
                calls.append((c, ["%s%d" % (kind, half[d])], [piece(kind, half[d], [on[k][d]])]))
    for kind in "sc":
        for k in chips:
            for d, o in ((db, dr), (dr, db)):
                calls.append((on[k][d], ["%s%d" % (kind, half[d])], [piece(kind, half[d], [on[k][o]])]))
    return root, calls


def masks(topo, src, xf):
    used, out = 0, []
    for kind, a, b, dsts, grp in xf:
        m = topo.mask(src, dsts[0])
        for d in dsts:
            m &= topo.mask(src, d)
        m &= ~used
        used |= m
        out.append((m, sum(m >> e & 1 for e in range(m.bit_length()))))
    return out


def rank_program(g, core, T, topo):
    root, calls = build_plan(T, topo)
    rank = T.rank_of(core)

    def view(kind, a, b):
        return T.wq[:, a:b].bitcast(dt.uint8) if kind == "c" else T.ws[:, a:b]

    expect, cover = {}, []
    for src, need, xf in calls:
        for (kind, a, b, dsts, grp), (m, n) in zip(xf, masks(topo, src, xf)):
            if core in dsts:
                expect[grp] = expect.get(grp, 0) + n
                cover.append((a, b, grp))
    mine = [c for c in calls if c[0] == core]
    if rank is None and not mine:
        return

    xst = HALVES if core == root else [(0, NW)]
    if core == root:
        for k, (a, b) in enumerate(HALVES):
            q = g.sync if k % 2 == 0 else g.scalar
            q.dma_start(T.wb[:, 4 * a:4 * b], T.w[:, 4 * a:4 * b]).then_inc(T.sem["wl%d" % k], 16)
        for k, (a, b) in enumerate(HALVES):
            g.vector.wait_ge(T.sem["wl%d" % k], 16)
            g.vector.quantize_mx(T.wq[:, a:b], T.ws[:, a:b], T.wb[:, 4 * a:4 * b]).then_inc(T.sem["q%d" % k], 1)
    if rank is not None:
        for k, (a, b) in enumerate(xst):
            if core == root and k == len(xst) - 1:
                g.sync.wait_ge(T.sem.go, 1)
            g.sync.dma_start(T.xb[:, 4 * a:4 * b], T.x[:, 4 * a:4 * b]).then_inc(T.sem["xl%d" % k], 16)
        for k, (a, b) in enumerate(xst):
            g.vector.wait_ge(T.sem["xl%d" % k], 16)
            g.vector.quantize_mx(T.xq[:, a:b], T.xs[:, a:b], T.xb[:, 4 * a:4 * b]).then_inc(T.sem["xq%d" % k], 1)

    left = 0
    for src, need, xf in mine:
        for s in need:
            g.wait_ge(T.sem[s], 1 if core == root else expect[s])
        trs = []
        for (kind, a, b, dsts, grp), (m, n) in zip(xf, masks(topo, core, xf)):
            ids = []
            for d in dsts:
                rid, pid = topo.addr(d, core)
                ids.append(DstId(rid=rid, pnc=pid))
            trs.append(RemoteDMATransfer(dst_ids=ids, dma_engine_mask=m, remote_sem=T.sem[grp],
                                         srcs=[view(kind, a, b)], dsts=[view(kind, a, b) for d in dsts]))
            left += n
        g.remote_dma_fused(trs, local_sem=T.sem.sent)
    if core == root:
        g.sem_inc(T.sem.go, 1)
    if left:
        g.wait_ge(T.sem.sent, left)
    if rank is None:
        return

    te = g.tensor
    order = []
    for t in range(KT):
        a, b = t * TW, (t + 1) * TW
        if core == root:
            needs = [(k, "q%d" % k, 1) for k, (sa, sb) in enumerate(HALVES) if sa < b and a < sb]
        else:
            needs = [(i, grp, expect[grp]) for i, (ca, cb, grp) in enumerate(cover) if ca < b and a < cb]
        first = max(needs)[0]
        needs = needs + [(k, "xq%d" % k, 1) for k, (sa, sb) in enumerate(xst) if sa < b and a < sb]
        order.append((first, t, needs))
    order.sort()
    seen = set()
    last = None
    for j, (_, t, needs) in enumerate(order):
        for _i, s, v in needs:
            if s not in seen:
                seen.add(s)
                te.wait_ge(T.sem[s], v)
        a, b = t * TW, (t + 1) * TW
        last = te.matmul_mx(T.acc[:, 0:TW], T.wq[:, a:b], T.ws[:, a:b], T.xq[:, a:b], T.xs[:, a:b], j == 0, j == KT - 1)
    last.then_inc(T.sem.mm, 1)
    g.vector.wait_ge(T.sem.mm, 1)
    g.vector.tensor_copy(T.yo[:], T.acc[:, 0:TW]).then_inc(T.sem.cp, 1)
    g.sync.wait_ge(T.sem.cp, 1)
    g.sync.dma_start(T.y[:], T.yo[:]).then_inc(T.sem.st, 16)
    g.sync.wait_ge(T.sem.st, 16)
